import numpy as np
import ml_dtypes


def mxq(x, axis, fmt="e4m3"):
    dtype, down = {"e4m3": (ml_dtypes.float8_e4m3fn, 7), "e5m2": (ml_dtypes.float8_e5m2, 14)}[fmt]
    v = np.moveaxis(np.asarray(x, np.float32).astype(ml_dtypes.bfloat16).astype(np.float64), axis, -1)
    blocks = v.reshape(v.shape[:-1] + (-1, 32))
    amax = np.abs(blocks).max(-1, keepdims=True)
    byte = np.maximum(np.where(amax > 0, np.frexp(amax)[1] - 1 + 127, 0) - down, 1)
    scale = np.exp2(byte - 127.0)
    codes = (blocks / scale).astype(np.float32).astype(dtype).astype(np.float64)
    return np.moveaxis((codes * scale).reshape(v.shape), -1, axis)


WIDE = False


def mx_kscale(k):
    if not WIDE:
        return np.ones(k)
    levels = np.array([10, -10, 5, -5, 0])
    if k % 512:
        return np.exp2(np.random.permutation(np.resize(levels, k // 32))).repeat(32)
    a = np.empty((k // 512, 16))
    for p in range(k // 512):
        a[p, :8] = np.random.permutation(np.resize(levels, 8))
        for g in range(8):
            far = levels[np.abs(levels - a[p, g]) >= 10]
            a[p, g + 8] = far[np.random.randint(len(far))]
    return np.exp2(a.ravel()).repeat(32)


def f64(x):
    return np.asarray(x).astype(np.float64)


def striped(idx):
    return np.tile(idx.reshape(-1, 16).T, (8, 1)).astype(np.uint16)


def unstriped(offs):
    return offs[:16].T.reshape(-1).astype(np.int64)


def striped8(idx):
    return np.concatenate([x.reshape(-1, 16).T for x in idx]).astype(np.uint16)


def runs(offs, k):
    lists = np.stack([offs[16 * r : 16 * r + 16].T.reshape(-1) for r in range(8)]).astype(np.int64)
    return lists[np.arange(k) % 512 // 64]


def pack_weight(w):
    k, n = w.shape
    w = f64(np.asarray(w, np.float32).astype(ml_dtypes.bfloat16)).reshape(k // 32, 32, n)
    amax = np.abs(w).max(1)
    byte = np.clip(np.where(amax > 0, np.frexp(amax)[1] - 1 + 127 - 7, 1), 1, 254)
    scaled = (w * np.exp2(127.0 - byte)[:, None, :]).reshape(k, n).astype(np.float32)
    words = np.ascontiguousarray(scaled.reshape(k // 512, 128, 4, n).transpose(0, 1, 3, 2)).astype(ml_dtypes.float8_e4m3fn).view(np.uint8)
    return words, np.ascontiguousarray(byte.astype(np.uint8).reshape(k // 512, 16, n))


def unpack_weight(words, scales):
    g, p, n, _ = words.shape
    vals = np.ascontiguousarray(words).view(ml_dtypes.float8_e4m3fn).astype(np.float64) * np.repeat(np.exp2(scales.astype(np.float64) - 127.0), 8, axis=1)[..., None]
    return vals.transpose(0, 1, 3, 2).reshape(g * 512, n)


K, T, S, N, G, H, W, U = 512, 1024, 512, 512, 2048, 512, 256, 384


def setup_inputs():
    n = np.random.standard_normal
    s = mx_kscale(K)[:, None]
    u = mx_kscale(S)
    packed_xT = pack_weight(n((K, T)) * s)
    packed_dT = pack_weight(n((K, G)) / s)
    return {
        "x_words": packed_xT[0],
        "x_scales": packed_xT[1],
        "d_words": packed_dT[0],
        "d_scales": packed_dT[1],
        "gn": (np.random.uniform(0.5, 1.5, (H, 1)) * u[:, None]).astype(np.float32),
        "w1": (n((H, N)) / np.sqrt(H) / u[:, None]).astype(np.float32),
        "offs": striped(np.random.permutation(T)[:S]),
        "k1": striped8(np.random.randint(0, G, (8, H))),
        "two": striped(np.random.permutation(T)[:S]),
        "k2": striped8(np.random.randint(0, G, (8, H))),
        "n1": striped(np.random.permutation(S)[:W]),
        "n2": striped(np.random.permutation(S)[:W]),
        "n3": striped(np.random.permutation(S)[:U]),
        "n4": striped(np.random.permutation(S)[:U]),
    }


def reference(x_words, x_scales, d_words, d_scales, gn, w1, offs, k1, two, k2, n1, n2, n3, n4):
    d_k2 = unpack_weight(d_words, d_scales)[np.arange(K)[:, None], runs(k2, K)]
    x_two = unpack_weight(x_words, x_scales)[:, unstriped(two)]
    b = 0.0625 * (d_k2.T @ x_two)
    d_k1 = unpack_weight(d_words, d_scales)[np.arange(K)[:, None], runs(k1, K)]
    xq = unpack_weight(x_words, x_scales)[:, unstriped(offs)]
    a = 0.0625 * (d_k1.T @ xq)
    ra = b[:, unstriped(n2)] - (0.5 * a[:, unstriped(n1)])
    ds = a.copy()
    ds[:, unstriped(n1)] = ra
    z = f64(gn) * ds
    h = mxq(f64(w1), 0, "e4m3").T @ mxq(z, 0, "e4m3")
    old = h[:, unstriped(n3)]
    pa = h[:, unstriped(n4)]
    ra2 = old - np.tanh(pa)
    out = h.copy()
    out[:, unstriped(n3)] = ra2
    return out

@@ -1,0 +1,267 @@
+from contextlib import ExitStack
+
+import concourse.mybir as mybir
+
+K, T, S, N, G, H, W, U = 512, 1024, 512, 512, 2048, 512, 256, 384
+FLOPS = 2 * K * H * S * 2 + 2 * H * N * S
+
+F32 = mybir.dt.float32
+BF16 = mybir.dt.bfloat16
+I32 = mybir.dt.int32
+U32 = mybir.dt.uint32
+U16 = mybir.dt.uint16
+U8 = mybir.dt.uint8
+FP8X4 = mybir.dt.float8_e4m3fn_x4
+MULT = mybir.AluOpType.mult
+ADD = mybir.AluOpType.add
+COPY = mybir.ActivationFunctionType.Copy
+TANH = mybir.ActivationFunctionType.Tanh
+
+P = 128
+PACK = 4
+ROWS = 16
+SUB = 8
+
+
+def tile_picked_twpqputbktanh_none_p_kernel(
+    tc, x_words, x_scales, d_words, d_scales, gn, w1, offs, k1, two, k2, n1, n2, n3, n4, out
+):
+    nc = tc.nc
+    with ExitStack() as ctx:
+        lists = ctx.enter_context(tc.tile_pool(name="lists", bufs=1))
+        sb = ctx.enter_context(tc.tile_pool(name="sb", bufs=1))
+        psum = ctx.enter_context(tc.psum_pool(name="psum", bufs=1))
+
+        def load_list(name, src):
+            t = lists.tile(list(src.shape), U16, name=name)
+            nc.sync.dma_start(t[:], src)
+            return t
+
+        def load_scale_rows(name, src, width):
+            t = sb.tile([P, width], U8, name=name, align_bytes=64)
+            rows = src[0].bitcast(I32).unsqueeze(1).to_broadcast([ROWS, SUB, width // 4])
+            nc.sync.dma_start(t[:].bitcast(I32), rows)
+            return t
+
+        def load_words(name, src, width):
+            t = sb.tile([P, width], U32, name=name, align_bytes=64)
+            nc.sync.dma_start(t[:].bitcast(I32), src[0].rearrange("p n t -> p (n t)").bitcast(I32))
+            return t
+
+        k1_t = load_list("k1_t", k1)
+        d_bytes = load_scale_rows("d_bytes", d_scales, G)
+        k2_t = load_list("k2_t", k2)
+        offs_t = load_list("offs_t", offs)
+        x_bytes = sb.tile([P, T], U8, name="x_bytes", tag="x_bytes", align_bytes=64)
+        for q in range(4):
+            rows = x_scales[0, 4 * q : 4 * q + 4, :].bitcast(I32).unsqueeze(0).to_broadcast([SUB, 4, T // 4])
+            queue = nc.sync if q < 2 else nc.gpsimd
+            queue.dma_start(x_bytes[32 * q : 32 * q + 32, :].bitcast(I32), rows)
+        x_win = load_words("x_win", x_words, T)
+        d_win = load_words("d_win", d_words, G)
+
+        w_rows = w1.rearrange("(q t r) m -> t q r m", t=PACK, r=SUB)
+        w_raw = []
+
+        def load_w(c, tag):
+            raw = sb.tile([P, PACK, N // 2], F32, name="w_raw%d" % c, tag=tag, align_bytes=64)
+            for t in range(PACK):
+                nc.sync.dma_start(raw[:, t, :], w_rows[t, :, :, c * (N // 2) : (c + 1) * (N // 2)])
+            w_raw.append(raw)
+
+        load_w(0, "w_raw0")
+        two_t = load_list("two_t", two)
+        n1_t = load_list("n1_t", n1)
+        planes = sb.tile([P, 2, H], U8, name="planes", align_bytes=64)
+        planes_flat = planes[:].rearrange("p c s -> p (c s)").bitcast(I32)
+        nc.vector.memset(planes_flat, 0)
+        gain_raw = sb.tile([P, PACK, 8], F32, name="gain_raw")
+        gn_rows = gn.rearrange("(q t r) o -> t q r o", t=PACK, r=SUB)
+        with nc.allow_non_contiguous_dma(reason="one gain a row"):
+            for t in range(PACK):
+                nc.gpsimd.dma_start(gain_raw[:, t, 0:1], gn_rows[t])
+        gain = sb.tile([P, PACK], F32, name="gain")
+        nc.gpsimd.tensor_scalar(gain[:], gain_raw[:, :, 0], 0.0625, 0.0, MULT, ADD)
+
+        picked = sb.tile([P, 2, H], U8, name="picked", tag="picked", align_bytes=64)
+        for c, lst in enumerate((k1_t, k2_t)):
+            nc.vector.tensor_copy(picked[:, c, :], d_bytes[:].indirect(lst[:]))
+        staged = sb.tile([P, 2, H], U8, name="staged", tag="staged", align_bytes=64)
+        for c in range(2):
+            nc.vector.tensor_copy(
+                staged[:, c, :].bitcast(I32).rearrange("p (t q r) -> p t q r", t=PACK, r=2),
+                picked[:, c, :].bitcast(I32).rearrange("p (q t r) -> p t q r", t=PACK, r=2),
+            )
+        flat = staged[:].rearrange("p c s -> p (c s)").bitcast(I32)
+        for q in range(4):
+            nc.sync.dma_start(planes_flat[32 * q : 32 * q + 4, :], flat[32 * q : 32 * q + 32 : SUB, :])
+        n2_t = load_list("n2_t", n2)
+        n4_t = load_list("n4_t", n4)
+        n3_t = load_list("n3_t", n3)
+
+        w_codes = [sb.tile([P, N // 2], U32, name="w_codes%d" % c, align_bytes=64) for c in range(2)]
+        w_plane = [sb.tile([P, N // 2], U8, name="w_plane%d" % c, align_bytes=64) for c in range(2)]
+        w_bf = []
+
+        def round_w(c, tag):
+            t = sb.tile([P, N // 2, PACK], BF16, name="w_bf%d" % c, tag=tag, align_bytes=64)
+            nc.scalar.activation(t[:], w_raw[c][:].rearrange("p t m -> p m t"), COPY)
+            w_bf.append(t)
+
+        def quant_w(c):
+            nc.vector.quantize_mx(
+                out=w_codes[c][:].bitcast(FP8X4), scales=w_plane[c][:], in_=w_bf[c][:].rearrange("p m t -> p (m t)")
+            )
+
+        round_w(0, "w_bf0")
+
+        banks = [psum.tile([P, S], F32, name="bank%d" % b, tag="bank%d" % b) for b in range(8)]
+
+        def product(name, d_list, x_list, d_picked, x_codes, x_plane, d_plane, outs):
+            nc.vector.tensor_copy(x_plane[:], x_bytes[:].indirect(x_list[:]))
+            nc.vector.tensor_copy(x_codes, x_win[:].indirect(x_list[:]))
+            nc.vector.tensor_copy(d_picked, d_win[:].indirect(d_list[:]))
+            d_codes = sb.tile([P, H], U32, name=name + "_d", tag="dealt", align_bytes=64)
+            nc.vector.tensor_copy(
+                d_codes[:].rearrange("p (t q r) -> p t q r", t=PACK, r=SUB),
+                d_picked.rearrange("p (q t r) -> p t q r", t=PACK, r=SUB),
+            )
+            for t in range(PACK):
+                cols = slice(t * P, (t + 1) * P)
+                nc.tensor.matmul_mx(
+                    out=outs[t][:],
+                    lhsT=d_codes[:, cols].bitcast(FP8X4),
+                    lhsT_scale=planes[:, d_plane, cols],
+                    rhs=x_codes.bitcast(FP8X4),
+                    rhs_scale=x_plane[:],
+                    start=True,
+                    stop=True,
+                )
+
+        a_x = sb.tile([P, S], U32, name="a_x", align_bytes=64)
+        a_dp = sb.tile([P, H], U32, name="a_dp", tag="gathered", align_bytes=64)
+        a_xp = sb.tile([P, S], U8, name="a_xp", align_bytes=64)
+        product("a", k1_t, offs_t, a_dp[:], a_x[:], a_xp, 0, banks[0:4])
+        ds = []
+        half = []
+        for t in range(PACK):
+            a_t = sb.tile([P, S], F32, name="ds%d" % t)
+            nc.scalar.activation(a_t[:], banks[t][:], COPY, scale=gain[:, t : t + 1])
+            h_t = sb.tile([P, W], F32, name="half%d" % t)
+            nc.scalar.activation(h_t[:], a_t[:].indirect(n1_t[:]), COPY, scale=-0.5)
+            ds.append(a_t)
+            half.append(h_t)
+
+        b_both = sb.tile([P, 2, S], U32, name="b_both", tag="gathered", align_bytes=64)
+        b_xp = sb.tile([P, S], U8, name="b_xp", tag="staged", align_bytes=64)
+        product("b", k2_t, two_t, b_both[:, 0, :], b_both[:, 1, :], b_xp, 1, banks[4:8])
+        quant_w(0)
+        load_w(1, "x_bytes")
+
+        b_sb = [sb.tile([P, S], F32, name="b%d" % t) for t in range(PACK)]
+        ra = [sb.tile([P, W], F32, name="ra%d" % t, tag="ra%d" % t, align_bytes=64) for t in range(PACK)]
+
+        def b_out(t):
+            nc.vector.tensor_scalar(b_sb[t][:], banks[4 + t][:], gain[:, t : t + 1], None, MULT)
+
+        def b_fetch(t):
+            nc.vector.tensor_tensor(ra[t][:], b_sb[t][:].indirect(n2_t[:]), half[t][:], ADD)
+
+        pairs = sb.tile([P, 2, S, 2], BF16, name="pairs", align_bytes=64)
+
+        def round_z(t):
+            nc.vector.tensor_copy(pairs[:, t // 2, :, t % 2], ds[t][:])
+
+        nc.scalar.activation(b_sb[0][:], banks[4][:], COPY, scale=gain[:, 0:1])
+        nc.scalar.activation(ra[0][:], b_sb[0][:].indirect(n2_t[:]), COPY)
+        b_out(1)
+        b_fetch(1)
+        b_out(2)
+        b_out(3)
+        b_fetch(2)
+        b_fetch(3)
+        for t in range(1, 4):
+            nc.scalar.activation(ds[t][:].indirect(n1_t[:]), ra[t][:], COPY)
+        nc.vector.tensor_tensor(ds[0][:].indirect(n1_t[:]), ra[0][:], half[0][:], ADD)
+        for t in range(PACK):
+            round_z(t)
+        round_w(1, "ra3")
+
+        z_bf = sb.tile([P, S, PACK], BF16, name="z_bf", align_bytes=64)
+        z_codes = sb.tile([P, S], U32, name="z_codes", align_bytes=64)
+        z_plane = sb.tile([P, S], U8, name="z_plane", align_bytes=64)
+        pair_words = pairs[:].rearrange("p h s e -> p h (s e)").bitcast(I32)
+        z_words = z_bf[:].rearrange("p s t -> p (s t)").bitcast(I32).rearrange("p (s h) -> p s h", h=2)
+        halves = [slice(0, S // 2), slice(S // 2, S)]
+        for cols in halves:
+            nc.vector.tensor_copy(z_words[:, cols, :], pair_words[:, :, cols].rearrange("p h s -> p s h"))
+        for cols in halves:
+            nc.vector.quantize_mx(
+                out=z_codes[:, cols].bitcast(FP8X4),
+                scales=z_plane[:, cols],
+                in_=z_bf[:, cols, :].rearrange("p s t -> p (s t)"),
+            )
+
+        quant_w(1)
+
+        h_banks = [psum.tile([P, S], F32, name="h%d" % m, tag="bank%d" % m) for m in range(4)]
+        for m in range(4):
+            cols = slice(m % 2 * P, (m % 2 + 1) * P)
+            nc.tensor.matmul_mx(
+                out=h_banks[m][:],
+                lhsT=w_codes[m // 2][:, cols].bitcast(FP8X4),
+                lhsT_scale=w_plane[m // 2][:, cols],
+                rhs=z_codes[:].bitcast(FP8X4),
+                rhs_scale=z_plane[:],
+                start=True,
+                stop=True,
+            )
+
+        h_sb = [sb.tile([P, S], F32, name="h_sb%d" % m) for m in range(4)]
+        pa = [sb.tile([P, U], F32, name="pa%d" % m) for m in range(4)]
+        th = [sb.tile([P, U], F32, name="th%d" % m) for m in range(4)]
+        ra2 = [sb.tile([P, U], F32, name="ra2_%d" % m) for m in range(4)]
+
+        def h_out(m):
+            nc.scalar.copy(h_sb[m][:], h_banks[m][:])
+
+        def pa_s(m):
+            nc.scalar.activation(pa[m][:], h_sb[m][:].indirect(n4_t[:]), COPY)
+
+        def pa_v(m):
+            nc.vector.tensor_copy(pa[m][:], h_sb[m][:].indirect(n4_t[:]))
+
+        def tanh(m):
+            nc.scalar.activation(th[m][:], pa[m][:], TANH, scale=-1.0)
+
+        def old(m):
+            nc.vector.tensor_tensor(ra2[m][:], h_sb[m][:].indirect(n3_t[:]), th[m][:], ADD)
+
+        def put_s(m):
+            nc.scalar.activation(h_sb[m][:].indirect(n3_t[:]), ra2[m][:], COPY)
+            nc.sync.dma_start(out[m * P : (m + 1) * P, :], h_sb[m][:])
+
+        def put_v(m):
+            nc.vector.tensor_copy(h_sb[m][:].indirect(n3_t[:]), ra2[m][:])
+            nc.sync.dma_start(out[m * P : (m + 1) * P, :], h_sb[m][:])
+
+        h_out(0)
+        pa_v(0)
+        h_out(1)
+        pa_v(1)
+        tanh(0)
+        h_out(2)
+        old(0)
+        tanh(1)
+        h_out(3)
+        old(1)
+        pa_s(2)
+        tanh(2)
+        put_v(0)
+        pa_s(3)
+        tanh(3)
+        old(2)
+        put_s(1)
+        old(3)
+        put_s(2)
+        put_v(3)

@@ -1,6 +1,7 @@
 from contextlib import ExitStack
 
 import concourse.mybir as mybir
+from concourse.masks import make_identity
 
 K, T, S, N, G, H, W, U = 512, 1024, 512, 512, 2048, 512, 256, 384
 FLOPS = 2 * K * H * S * 2 + 2 * H * N * S
@@ -50,48 +51,42 @@ def tile_picked_twpqputbktanh_none_p_kernel(
 
         k1_t = load_list("k1_t", k1)
         d_bytes = load_scale_rows("d_bytes", d_scales, G)
-        k2_t = load_list("k2_t", k2)
-        offs_t = load_list("offs_t", offs)
         x_bytes = sb.tile([P, T], U8, name="x_bytes", tag="x_bytes", align_bytes=64)
         for q in range(4):
             rows = x_scales[0, 4 * q : 4 * q + 4, :].bitcast(I32).unsqueeze(0).to_broadcast([SUB, 4, T // 4])
-            queue = nc.sync if q < 2 else nc.gpsimd
-            queue.dma_start(x_bytes[32 * q : 32 * q + 32, :].bitcast(I32), rows)
+            nc.sync.dma_start(x_bytes[32 * q : 32 * q + 32, :].bitcast(I32), rows)
+        k2_t = load_list("k2_t", k2)
         x_win = load_words("x_win", x_words, T)
-        d_win = load_words("d_win", d_words, G)
-
-        w_rows = w1.rearrange("(q t r) m -> t q r m", t=PACK, r=SUB)
-        w_raw = []
-
-        def load_w(c, tag):
-            raw = sb.tile([P, PACK, N // 2], F32, name="w_raw%d" % c, tag=tag, align_bytes=64)
-            for t in range(PACK):
-                nc.sync.dma_start(raw[:, t, :], w_rows[t, :, :, c * (N // 2) : (c + 1) * (N // 2)])
-            w_raw.append(raw)
-
-        load_w(0, "w_raw0")
+        offs_t = load_list("offs_t", offs)
         two_t = load_list("two_t", two)
         n1_t = load_list("n1_t", n1)
+        d_win = load_words("d_win", d_words, G)
         planes = sb.tile([P, 2, H], U8, name="planes", align_bytes=64)
         planes_flat = planes[:].rearrange("p c s -> p (c s)").bitcast(I32)
         nc.vector.memset(planes_flat, 0)
-        gain_raw = sb.tile([P, PACK, 8], F32, name="gain_raw")
-        gn_rows = gn.rearrange("(q t r) o -> t q r o", t=PACK, r=SUB)
-        with nc.allow_non_contiguous_dma(reason="one gain a row"):
-            for t in range(PACK):
-                nc.gpsimd.dma_start(gain_raw[:, t, 0:1], gn_rows[t])
+        banks = [psum.tile([P, S], F32, name="bank%d" % b, tag="bank%d" % b) for b in range(7)]
+        gain_rows = sb.tile([P, P], F32, name="gain_rows")
+        nc.gpsimd.memset(gain_rows[:], 0.0)
+        nc.gpsimd.dma_start(
+            gain_rows[0:PACK, :].rearrange("t (q r) -> t q r", r=SUB),
+            gn.rearrange("(q t r) o -> t q (r o)", t=PACK, r=SUB),
+        )
+        ident = sb.tile([P, P], F32, name="ident")
+        make_identity(nc, ident[:])
+        gain_ps = psum.tile([P, P], F32, name="gain_ps", tag="bank7")
+        nc.tensor.transpose(gain_ps[:], gain_rows[:], ident[:])
         gain = sb.tile([P, PACK], F32, name="gain")
-        nc.gpsimd.tensor_scalar(gain[:], gain_raw[:, :, 0], 0.0625, 0.0, MULT, ADD)
+        nc.scalar.activation(gain[:], gain_ps[:, 0:PACK], COPY, scale=0.0625)
+        banks.append(psum.tile([P, S], F32, name="bank7", tag="bank7"))
 
-        picked = sb.tile([P, 2, H], U8, name="picked", tag="picked", align_bytes=64)
+        picked = sb.tile([P, 2, H], U8, name="picked", align_bytes=64)
         for c, lst in enumerate((k1_t, k2_t)):
             nc.vector.tensor_copy(picked[:, c, :], d_bytes[:].indirect(lst[:]))
         staged = sb.tile([P, 2, H], U8, name="staged", tag="staged", align_bytes=64)
-        for c in range(2):
-            nc.vector.tensor_copy(
-                staged[:, c, :].bitcast(I32).rearrange("p (t q r) -> p t q r", t=PACK, r=2),
-                picked[:, c, :].bitcast(I32).rearrange("p (q t r) -> p t q r", t=PACK, r=2),
-            )
+        nc.vector.tensor_copy(
+            staged[:].bitcast(I32).rearrange("p c (t q r) -> p c t q r", t=PACK, r=2),
+            picked[:].bitcast(I32).rearrange("p c (q t r) -> p c t q r", t=PACK, r=2),
+        )
         flat = staged[:].rearrange("p c s -> p (c s)").bitcast(I32)
         for q in range(4):
             nc.sync.dma_start(planes_flat[32 * q : 32 * q + 4, :], flat[32 * q : 32 * q + 32 : SUB, :])
@@ -99,29 +94,11 @@ def tile_picked_twpqputbktanh_none_p_kernel(
         n4_t = load_list("n4_t", n4)
         n3_t = load_list("n3_t", n3)
 
-        w_codes = [sb.tile([P, N // 2], U32, name="w_codes%d" % c, align_bytes=64) for c in range(2)]
-        w_plane = [sb.tile([P, N // 2], U8, name="w_plane%d" % c, align_bytes=64) for c in range(2)]
-        w_bf = []
-
-        def round_w(c, tag):
-            t = sb.tile([P, N // 2, PACK], BF16, name="w_bf%d" % c, tag=tag, align_bytes=64)
-            nc.scalar.activation(t[:], w_raw[c][:].rearrange("p t m -> p m t"), COPY)
-            w_bf.append(t)
-
-        def quant_w(c):
-            nc.vector.quantize_mx(
-                out=w_codes[c][:].bitcast(FP8X4), scales=w_plane[c][:], in_=w_bf[c][:].rearrange("p m t -> p (m t)")
-            )
-
-        round_w(0, "w_bf0")
-
-        banks = [psum.tile([P, S], F32, name="bank%d" % b, tag="bank%d" % b) for b in range(8)]
-
         def product(name, d_list, x_list, d_picked, x_codes, x_plane, d_plane, outs):
             nc.vector.tensor_copy(x_plane[:], x_bytes[:].indirect(x_list[:]))
-            nc.vector.tensor_copy(x_codes, x_win[:].indirect(x_list[:]))
             nc.vector.tensor_copy(d_picked, d_win[:].indirect(d_list[:]))
-            d_codes = sb.tile([P, H], U32, name=name + "_d", tag="dealt", align_bytes=64)
+            nc.vector.tensor_copy(x_codes, x_win[:].indirect(x_list[:]))
+            d_codes = sb.tile([P, H], U32, name=name + "_d", align_bytes=64)
             nc.vector.tensor_copy(
                 d_codes[:].rearrange("p (t q r) -> p t q r", t=PACK, r=SUB),
                 d_picked.rearrange("p (q t r) -> p t q r", t=PACK, r=SUB),
@@ -153,10 +130,16 @@ def tile_picked_twpqputbktanh_none_p_kernel(
             half.append(h_t)
 
         b_both = sb.tile([P, 2, S], U32, name="b_both", tag="gathered", align_bytes=64)
-        b_xp = sb.tile([P, S], U8, name="b_xp", tag="staged", align_bytes=64)
+        b_xp = sb.tile([P, S], U8, name="b_xp", align_bytes=64)
         product("b", k2_t, two_t, b_both[:, 0, :], b_both[:, 1, :], b_xp, 1, banks[4:8])
-        quant_w(0)
-        load_w(1, "x_bytes")
+        w_rows = w1.rearrange("(q t r) m -> t q r m", t=PACK, r=SUB)
+        halves = [slice(0, S // 2), slice(S // 2, S)]
+        w_raw = []
+        for c, tag in enumerate(("x_bytes", "staged")):
+            raw = sb.tile([P, PACK, N // 2], F32, name="w_raw%d" % c, tag=tag, align_bytes=64)
+            for t in range(PACK):
+                nc.sync.dma_start(raw[:, t, :], w_rows[t, :, :, halves[c]])
+            w_raw.append(raw)
 
         b_sb = [sb.tile([P, S], F32, name="b%d" % t) for t in range(PACK)]
         ra = [sb.tile([P, W], F32, name="ra%d" % t, tag="ra%d" % t, align_bytes=64) for t in range(PACK)]
@@ -172,50 +155,70 @@ def tile_picked_twpqputbktanh_none_p_kernel(
         def round_z(t):
             nc.vector.tensor_copy(pairs[:, t // 2, :, t % 2], ds[t][:])
 
-        nc.scalar.activation(b_sb[0][:], banks[4][:], COPY, scale=gain[:, 0:1])
-        nc.scalar.activation(ra[0][:], b_sb[0][:].indirect(n2_t[:]), COPY)
+        b_out(0)
+        b_fetch(0)
         b_out(1)
-        b_fetch(1)
         b_out(2)
+        b_fetch(1)
         b_out(3)
         b_fetch(2)
         b_fetch(3)
-        for t in range(1, 4):
+        for t in range(3):
             nc.scalar.activation(ds[t][:].indirect(n1_t[:]), ra[t][:], COPY)
-        nc.vector.tensor_tensor(ds[0][:].indirect(n1_t[:]), ra[0][:], half[0][:], ADD)
-        for t in range(PACK):
-            round_z(t)
-        round_w(1, "ra3")
+        nc.vector.tensor_copy(ds[3][:].indirect(n1_t[:]), ra[3][:])
+        round_z(0)
+        round_z(1)
+        round_z(3)
+        round_z(2)
+        w_bf = []
+        for c, tag in enumerate(("ra2", "x_bytes")):
+            rounded = sb.tile([P, N // 2, PACK], BF16, name="w_bf%d" % c, tag=tag, align_bytes=64)
+            nc.scalar.activation(rounded[:], w_raw[c][:].rearrange("p t m -> p m t"), COPY)
+            w_bf.append(rounded)
+        w_codes = [sb.tile([P, N // 2], U32, name="w_codes%d" % c, align_bytes=64) for c in range(2)]
+        w_plane = [sb.tile([P, N // 2], U8, name="w_plane%d" % c, align_bytes=64) for c in range(2)]
 
-        z_bf = sb.tile([P, S, PACK], BF16, name="z_bf", align_bytes=64)
-        z_codes = sb.tile([P, S], U32, name="z_codes", align_bytes=64)
-        z_plane = sb.tile([P, S], U8, name="z_plane", align_bytes=64)
-        pair_words = pairs[:].rearrange("p h s e -> p h (s e)").bitcast(I32)
-        z_words = z_bf[:].rearrange("p s t -> p (s t)").bitcast(I32).rearrange("p (s h) -> p s h", h=2)
-        halves = [slice(0, S // 2), slice(S // 2, S)]
-        for cols in halves:
-            nc.vector.tensor_copy(z_words[:, cols, :], pair_words[:, :, cols].rearrange("p h s -> p s h"))
-        for cols in halves:
+        def quant_w(c):
             nc.vector.quantize_mx(
-                out=z_codes[:, cols].bitcast(FP8X4),
-                scales=z_plane[:, cols],
-                in_=z_bf[:, cols, :].rearrange("p s t -> p (s t)"),
+                out=w_codes[c][:].bitcast(FP8X4),
+                scales=w_plane[c][:],
+                in_=w_bf[c][:].rearrange("p m t -> p (m t)"),
             )
 
+        pair_words = pairs[:].rearrange("p h s e -> p h (s e)").bitcast(I32)
+        z_bf = [sb.tile([P, S // 2, PACK], BF16, name="z_bf%d" % c, align_bytes=64) for c in range(2)]
+        z_codes = [sb.tile([P, S // 2], U32, name="z_codes%d" % c, align_bytes=64) for c in range(2)]
+        z_plane = [sb.tile([P, S // 2], U8, name="z_plane%d" % c, align_bytes=64) for c in range(2)]
+        for c in range(2):
+            z_words = z_bf[c][:].rearrange("p s t -> p (s t)").bitcast(I32).rearrange("p (s h) -> p s h", h=2)
+            nc.vector.tensor_copy(z_words, pair_words[:, :, halves[c]].rearrange("p h s -> p s h"))
+
+        def quant_z(c):
+            nc.vector.quantize_mx(
+                out=z_codes[c][:].bitcast(FP8X4),
+                scales=z_plane[c][:],
+                in_=z_bf[c][:].rearrange("p s t -> p (s t)"),
+            )
+
+        quant_z(0)
+        quant_w(0)
+        quant_z(1)
         quant_w(1)
 
         h_banks = [psum.tile([P, S], F32, name="h%d" % m, tag="bank%d" % m) for m in range(4)]
-        for m in range(4):
-            cols = slice(m % 2 * P, (m % 2 + 1) * P)
-            nc.tensor.matmul_mx(
-                out=h_banks[m][:],
-                lhsT=w_codes[m // 2][:, cols].bitcast(FP8X4),
-                lhsT_scale=w_plane[m // 2][:, cols],
-                rhs=z_codes[:].bitcast(FP8X4),
-                rhs_scale=z_plane[:],
-                start=True,
-                stop=True,
-            )
+        for pair in range(2):
+            for c in range(2):
+                for i in range(2):
+                    cols = slice(i * P, (i + 1) * P)
+                    nc.tensor.matmul_mx(
+                        out=h_banks[2 * pair + i][:, halves[c]],
+                        lhsT=w_codes[pair][:, cols].bitcast(FP8X4),
+                        lhsT_scale=w_plane[pair][:, cols],
+                        rhs=z_codes[c][:].bitcast(FP8X4),
+                        rhs_scale=z_plane[c][:],
+                        start=True,
+                        stop=True,
+                    )
 
         h_sb = [sb.tile([P, S], F32, name="h_sb%d" % m) for m in range(4)]
         pa = [sb.tile([P, U], F32, name="pa%d" % m) for m in range(4)]

@@ -51,7 +51,7 @@ def tile_picked_twpqputbktanh_none_p_kernel(
 
         k1_t = load_list("k1_t", k1)
         d_bytes = load_scale_rows("d_bytes", d_scales, G)
-        x_bytes = sb.tile([P, T], U8, name="x_bytes", tag="x_bytes", align_bytes=64)
+        x_bytes = sb.tile([P, T], U8, name="x_bytes", align_bytes=64)
         for q in range(4):
             rows = x_scales[0, 4 * q : 4 * q + 4, :].bitcast(I32).unsqueeze(0).to_broadcast([SUB, 4, T // 4])
             nc.sync.dma_start(x_bytes[32 * q : 32 * q + 32, :].bitcast(I32), rows)
@@ -60,7 +60,37 @@ def tile_picked_twpqputbktanh_none_p_kernel(
         offs_t = load_list("offs_t", offs)
         two_t = load_list("two_t", two)
         n1_t = load_list("n1_t", n1)
+        n2_t = load_list("n2_t", n2)
+        n4_t = load_list("n4_t", n4)
+        n3_t = load_list("n3_t", n3)
         d_win = load_words("d_win", d_words, G)
+
+        halves = [slice(0, S // 2), slice(S // 2, S)]
+        w_rows = w1.rearrange("(q t r) m -> t q r m", t=PACK, r=SUB)
+        w_raw = []
+        w_bf = []
+        w_codes = [sb.tile([P, N // 2], U32, name="w_codes%d" % c, align_bytes=64) for c in range(2)]
+        w_plane = [sb.tile([P, N // 2], U8, name="w_plane%d" % c, align_bytes=64) for c in range(2)]
+
+        def load_w(c, tag):
+            raw = sb.tile([P, PACK, N // 2], F32, name="w_raw%d" % c, tag=tag, align_bytes=64)
+            for t in range(PACK):
+                nc.sync.dma_start(raw[:, t, :], w_rows[t, :, :, halves[c]])
+            w_raw.append(raw)
+
+        def round_w(c, tag):
+            rounded = sb.tile([P, N // 2, PACK], BF16, name="w_bf%d" % c, tag=tag, align_bytes=64)
+            nc.scalar.activation(rounded[:], w_raw[c][:].rearrange("p t m -> p m t"), COPY)
+            w_bf.append(rounded)
+
+        def quant_w(c):
+            nc.vector.quantize_mx(
+                out=w_codes[c][:].bitcast(FP8X4),
+                scales=w_plane[c][:],
+                in_=w_bf[c][:].rearrange("p m t -> p (m t)"),
+            )
+
+        load_w(0, "w_raw0")
         planes = sb.tile([P, 2, H], U8, name="planes", align_bytes=64)
         planes_flat = planes[:].rearrange("p c s -> p (c s)").bitcast(I32)
         nc.vector.memset(planes_flat, 0)
@@ -90,9 +120,6 @@ def tile_picked_twpqputbktanh_none_p_kernel(
         flat = staged[:].rearrange("p c s -> p (c s)").bitcast(I32)
         for q in range(4):
             nc.sync.dma_start(planes_flat[32 * q : 32 * q + 4, :], flat[32 * q : 32 * q + 32 : SUB, :])
-        n2_t = load_list("n2_t", n2)
-        n4_t = load_list("n4_t", n4)
-        n3_t = load_list("n3_t", n3)
 
         def product(name, d_list, x_list, d_picked, x_codes, x_plane, d_plane, outs):
             nc.vector.tensor_copy(x_plane[:], x_bytes[:].indirect(x_list[:]))
@@ -115,7 +142,8 @@ def tile_picked_twpqputbktanh_none_p_kernel(
                     stop=True,
                 )
 
-        a_x = sb.tile([P, S], U32, name="a_x", align_bytes=64)
+        round_w(0, "a_w")
+        a_x = sb.tile([P, S], U32, name="a_x", tag="a_x", align_bytes=64)
         a_dp = sb.tile([P, H], U32, name="a_dp", tag="gathered", align_bytes=64)
         a_xp = sb.tile([P, S], U8, name="a_xp", align_bytes=64)
         product("a", k1_t, offs_t, a_dp[:], a_x[:], a_xp, 0, banks[0:4])
@@ -130,16 +158,10 @@ def tile_picked_twpqputbktanh_none_p_kernel(
             half.append(h_t)
 
         b_both = sb.tile([P, 2, S], U32, name="b_both", tag="gathered", align_bytes=64)
-        b_xp = sb.tile([P, S], U8, name="b_xp", align_bytes=64)
+        b_xp = sb.tile([P, S], U8, name="b_xp", tag="staged", align_bytes=64)
         product("b", k2_t, two_t, b_both[:, 0, :], b_both[:, 1, :], b_xp, 1, banks[4:8])
-        w_rows = w1.rearrange("(q t r) m -> t q r m", t=PACK, r=SUB)
-        halves = [slice(0, S // 2), slice(S // 2, S)]
-        w_raw = []
-        for c, tag in enumerate(("x_bytes", "staged")):
-            raw = sb.tile([P, PACK, N // 2], F32, name="w_raw%d" % c, tag=tag, align_bytes=64)
-            for t in range(PACK):
-                nc.sync.dma_start(raw[:, t, :], w_rows[t, :, :, halves[c]])
-            w_raw.append(raw)
+        quant_w(0)
+        load_w(1, "a_x")
 
         b_sb = [sb.tile([P, S], F32, name="b%d" % t) for t in range(PACK)]
         ra = [sb.tile([P, W], F32, name="ra%d" % t, tag="ra%d" % t, align_bytes=64) for t in range(PACK)]
@@ -160,7 +182,7 @@ def tile_picked_twpqputbktanh_none_p_kernel(
         b_out(1)
         b_out(2)
         b_fetch(1)
-        b_out(3)
+        nc.scalar.activation(b_sb[3][:], banks[7][:], COPY, scale=gain[:, 3:4])
         b_fetch(2)
         b_fetch(3)
         for t in range(3):
@@ -170,20 +192,7 @@ def tile_picked_twpqputbktanh_none_p_kernel(
         round_z(1)
         round_z(3)
         round_z(2)
-        w_bf = []
-        for c, tag in enumerate(("ra2", "x_bytes")):
-            rounded = sb.tile([P, N // 2, PACK], BF16, name="w_bf%d" % c, tag=tag, align_bytes=64)
-            nc.scalar.activation(rounded[:], w_raw[c][:].rearrange("p t m -> p m t"), COPY)
-            w_bf.append(rounded)
-        w_codes = [sb.tile([P, N // 2], U32, name="w_codes%d" % c, align_bytes=64) for c in range(2)]
-        w_plane = [sb.tile([P, N // 2], U8, name="w_plane%d" % c, align_bytes=64) for c in range(2)]
-
-        def quant_w(c):
-            nc.vector.quantize_mx(
-                out=w_codes[c][:].bitcast(FP8X4),
-                scales=w_plane[c][:],
-                in_=w_bf[c][:].rearrange("p m t -> p (m t)"),
-            )
+        round_w(1, "ra2")
 
         pair_words = pairs[:].rearrange("p h s e -> p h (s e)").bitcast(I32)
         z_bf = [sb.tile([P, S // 2, PACK], BF16, name="z_bf%d" % c, align_bytes=64) for c in range(2)]
@@ -201,7 +210,6 @@ def tile_picked_twpqputbktanh_none_p_kernel(
             )
 
         quant_z(0)
-        quant_w(0)
         quant_z(1)
         quant_w(1)
 
@@ -249,8 +257,8 @@ def tile_picked_twpqputbktanh_none_p_kernel(
             nc.sync.dma_start(out[m * P : (m + 1) * P, :], h_sb[m][:])
 
         h_out(0)
+        nc.vector.tensor_copy(h_sb[1][:], h_banks[1][:])
         pa_v(0)
-        h_out(1)
         pa_v(1)
         tanh(0)
         h_out(2)

@@ -257,8 +257,8 @@ def tile_picked_twpqputbktanh_none_p_kernel(
             nc.sync.dma_start(out[m * P : (m + 1) * P, :], h_sb[m][:])
 
         h_out(0)
-        nc.vector.tensor_copy(h_sb[1][:], h_banks[1][:])
         pa_v(0)
+        h_out(1)
         pa_v(1)
         tanh(0)
         h_out(2)

from contextlib import ExitStack

import concourse.mybir as mybir
from concourse.masks import make_identity

K, T, S, N, G, H, W, U = 512, 1024, 512, 512, 2048, 512, 256, 384
FLOPS = 2 * K * H * S * 2 + 2 * H * N * S

F32 = mybir.dt.float32
BF16 = mybir.dt.bfloat16
I32 = mybir.dt.int32
U32 = mybir.dt.uint32
U16 = mybir.dt.uint16
U8 = mybir.dt.uint8
FP8X4 = mybir.dt.float8_e4m3fn_x4
MULT = mybir.AluOpType.mult
ADD = mybir.AluOpType.add
COPY = mybir.ActivationFunctionType.Copy
TANH = mybir.ActivationFunctionType.Tanh

P = 128
PACK = 4
ROWS = 16
SUB = 8


def tile_picked_twpqputbktanh_none_p_kernel(
    tc, x_words, x_scales, d_words, d_scales, gn, w1, offs, k1, two, k2, n1, n2, n3, n4, out
):
    nc = tc.nc
    with ExitStack() as ctx:
        lists = ctx.enter_context(tc.tile_pool(name="lists", bufs=1))
        sb = ctx.enter_context(tc.tile_pool(name="sb", bufs=1))
        psum = ctx.enter_context(tc.psum_pool(name="psum", bufs=1))

        def load_list(name, src):
            t = lists.tile(list(src.shape), U16, name=name)
            nc.sync.dma_start(t[:], src)
            return t

        def load_scale_rows(name, src, width):
            t = sb.tile([P, width], U8, name=name, align_bytes=64)
            rows = src[0].bitcast(I32).unsqueeze(1).to_broadcast([ROWS, SUB, width // 4])
            nc.sync.dma_start(t[:].bitcast(I32), rows)
            return t

        def load_words(name, src, width):
            t = sb.tile([P, width], U32, name=name, align_bytes=64)
            nc.sync.dma_start(t[:].bitcast(I32), src[0].rearrange("p n t -> p (n t)").bitcast(I32))
            return t

        k1_t = load_list("k1_t", k1)
        d_bytes = load_scale_rows("d_bytes", d_scales, G)
        x_bytes = sb.tile([P, T], U8, name="x_bytes", align_bytes=64)
        for q in range(4):
            rows = x_scales[0, 4 * q : 4 * q + 4, :].bitcast(I32).unsqueeze(0).to_broadcast([SUB, 4, T // 4])
            nc.sync.dma_start(x_bytes[32 * q : 32 * q + 32, :].bitcast(I32), rows)
        k2_t = load_list("k2_t", k2)
        x_win = load_words("x_win", x_words, T)
        offs_t = load_list("offs_t", offs)
        two_t = load_list("two_t", two)
        n1_t = load_list("n1_t", n1)
        n2_t = load_list("n2_t", n2)
        n4_t = load_list("n4_t", n4)
        n3_t = load_list("n3_t", n3)
        d_win = load_words("d_win", d_words, G)

        halves = [slice(0, S // 2), slice(S // 2, S)]
        w_rows = w1.rearrange("(q t r) m -> t q r m", t=PACK, r=SUB)
        w_raw = []
        w_bf = []
        w_codes = [sb.tile([P, N // 2], U32, name="w_codes%d" % c, align_bytes=64) for c in range(2)]
        w_plane = [sb.tile([P, N // 2], U8, name="w_plane%d" % c, align_bytes=64) for c in range(2)]

        def load_w(c, tag):
            raw = sb.tile([P, PACK, N // 2], F32, name="w_raw%d" % c, tag=tag, align_bytes=64)
            for t in range(PACK):
                nc.sync.dma_start(raw[:, t, :], w_rows[t, :, :, halves[c]])
            w_raw.append(raw)

        def round_w(c, tag):
            rounded = sb.tile([P, N // 2, PACK], BF16, name="w_bf%d" % c, tag=tag, align_bytes=64)
            nc.scalar.activation(rounded[:], w_raw[c][:].rearrange("p t m -> p m t"), COPY)
            w_bf.append(rounded)

        def quant_w(c):
            nc.vector.quantize_mx(
                out=w_codes[c][:].bitcast(FP8X4),
                scales=w_plane[c][:],
                in_=w_bf[c][:].rearrange("p m t -> p (m t)"),
            )

        load_w(0, "w_raw0")
        planes = sb.tile([P, 2, H], U8, name="planes", align_bytes=64)
        planes_flat = planes[:].rearrange("p c s -> p (c s)").bitcast(I32)
        nc.vector.memset(planes_flat, 0)
        banks = [psum.tile([P, S], F32, name="bank%d" % b, tag="bank%d" % b) for b in range(7)]
        gain_rows = sb.tile([P, P], F32, name="gain_rows")
        nc.gpsimd.memset(gain_rows[:], 0.0)
        nc.gpsimd.dma_start(
            gain_rows[0:PACK, :].rearrange("t (q r) -> t q r", r=SUB),
            gn.rearrange("(q t r) o -> t q (r o)", t=PACK, r=SUB),
        )
        ident = sb.tile([P, P], F32, name="ident")
        make_identity(nc, ident[:])
        gain_ps = psum.tile([P, P], F32, name="gain_ps", tag="bank7")
        nc.tensor.transpose(gain_ps[:], gain_rows[:], ident[:])
        gain = sb.tile([P, PACK], F32, name="gain")
        nc.scalar.activation(gain[:], gain_ps[:, 0:PACK], COPY, scale=0.0625)
        banks.append(psum.tile([P, S], F32, name="bank7", tag="bank7"))

        picked = sb.tile([P, 2, H], U8, name="picked", align_bytes=64)
        for c, lst in enumerate((k1_t, k2_t)):
            nc.vector.tensor_copy(picked[:, c, :], d_bytes[:].indirect(lst[:]))
        staged = sb.tile([P, 2, H], U8, name="staged", tag="staged", align_bytes=64)
        nc.vector.tensor_copy(
            staged[:].bitcast(I32).rearrange("p c (t q r) -> p c t q r", t=PACK, r=2),
            picked[:].bitcast(I32).rearrange("p c (q t r) -> p c t q r", t=PACK, r=2),
        )
        flat = staged[:].rearrange("p c s -> p (c s)").bitcast(I32)
        for q in range(4):
            nc.sync.dma_start(planes_flat[32 * q : 32 * q + 4, :], flat[32 * q : 32 * q + 32 : SUB, :])

        def product(name, d_list, x_list, d_picked, x_codes, x_plane, d_plane, outs):
            nc.vector.tensor_copy(x_plane[:], x_bytes[:].indirect(x_list[:]))
            nc.vector.tensor_copy(d_picked, d_win[:].indirect(d_list[:]))
            nc.vector.tensor_copy(x_codes, x_win[:].indirect(x_list[:]))
            d_codes = sb.tile([P, H], U32, name=name + "_d", align_bytes=64)
            nc.vector.tensor_copy(
                d_codes[:].rearrange("p (t q r) -> p t q r", t=PACK, r=SUB),
                d_picked.rearrange("p (q t r) -> p t q r", t=PACK, r=SUB),
            )
            for t in range(PACK):
                cols = slice(t * P, (t + 1) * P)
                nc.tensor.matmul_mx(
                    out=outs[t][:],
                    lhsT=d_codes[:, cols].bitcast(FP8X4),
                    lhsT_scale=planes[:, d_plane, cols],
                    rhs=x_codes.bitcast(FP8X4),
                    rhs_scale=x_plane[:],
                    start=True,
                    stop=True,
                )

        round_w(0, "a_w")
        a_x = sb.tile([P, S], U32, name="a_x", tag="a_x", align_bytes=64)
        a_dp = sb.tile([P, H], U32, name="a_dp", tag="gathered", align_bytes=64)
        a_xp = sb.tile([P, S], U8, name="a_xp", align_bytes=64)
        product("a", k1_t, offs_t, a_dp[:], a_x[:], a_xp, 0, banks[0:4])
        ds = []
        half = []
        for t in range(PACK):
            a_t = sb.tile([P, S], F32, name="ds%d" % t)
            nc.scalar.activation(a_t[:], banks[t][:], COPY, scale=gain[:, t : t + 1])
            h_t = sb.tile([P, W], F32, name="half%d" % t)
            nc.scalar.activation(h_t[:], a_t[:].indirect(n1_t[:]), COPY, scale=-0.5)
            ds.append(a_t)
            half.append(h_t)

        b_both = sb.tile([P, 2, S], U32, name="b_both", tag="gathered", align_bytes=64)
        b_xp = sb.tile([P, S], U8, name="b_xp", tag="staged", align_bytes=64)
        product("b", k2_t, two_t, b_both[:, 0, :], b_both[:, 1, :], b_xp, 1, banks[4:8])
        quant_w(0)
        load_w(1, "a_x")

        b_sb = [sb.tile([P, S], F32, name="b%d" % t) for t in range(PACK)]
        ra = [sb.tile([P, W], F32, name="ra%d" % t, tag="ra%d" % t, align_bytes=64) for t in range(PACK)]

        def b_out(t):
            nc.vector.tensor_scalar(b_sb[t][:], banks[4 + t][:], gain[:, t : t + 1], None, MULT)

        def b_fetch(t):
            nc.vector.tensor_tensor(ra[t][:], b_sb[t][:].indirect(n2_t[:]), half[t][:], ADD)

        pairs = sb.tile([P, 2, S, 2], BF16, name="pairs", align_bytes=64)

        def round_z(t):
            nc.vector.tensor_copy(pairs[:, t // 2, :, t % 2], ds[t][:])

        b_out(0)
        b_fetch(0)
        b_out(1)
        b_out(2)
        b_fetch(1)
        nc.scalar.activation(b_sb[3][:], banks[7][:], COPY, scale=gain[:, 3:4])
        b_fetch(2)
        b_fetch(3)
        for t in range(3):
            nc.scalar.activation(ds[t][:].indirect(n1_t[:]), ra[t][:], COPY)
        nc.vector.tensor_copy(ds[3][:].indirect(n1_t[:]), ra[3][:])
        round_z(0)
        round_z(1)
        round_z(3)
        round_z(2)
        round_w(1, "ra2")

        pair_words = pairs[:].rearrange("p h s e -> p h (s e)").bitcast(I32)
        z_bf = [sb.tile([P, S // 2, PACK], BF16, name="z_bf%d" % c, align_bytes=64) for c in range(2)]
        z_codes = [sb.tile([P, S // 2], U32, name="z_codes%d" % c, align_bytes=64) for c in range(2)]
        z_plane = [sb.tile([P, S // 2], U8, name="z_plane%d" % c, align_bytes=64) for c in range(2)]
        for c in range(2):
            z_words = z_bf[c][:].rearrange("p s t -> p (s t)").bitcast(I32).rearrange("p (s h) -> p s h", h=2)
            nc.vector.tensor_copy(z_words, pair_words[:, :, halves[c]].rearrange("p h s -> p s h"))

        def quant_z(c):
            nc.vector.quantize_mx(
                out=z_codes[c][:].bitcast(FP8X4),
                scales=z_plane[c][:],
                in_=z_bf[c][:].rearrange("p s t -> p (s t)"),
            )

        quant_z(0)
        quant_z(1)
        quant_w(1)

        h_banks = [psum.tile([P, S], F32, name="h%d" % m, tag="bank%d" % m) for m in range(4)]
        for pair in range(2):
            for c in range(2):
                for i in range(2):
                    cols = slice(i * P, (i + 1) * P)
                    nc.tensor.matmul_mx(
                        out=h_banks[2 * pair + i][:, halves[c]],
                        lhsT=w_codes[pair][:, cols].bitcast(FP8X4),
                        lhsT_scale=w_plane[pair][:, cols],
                        rhs=z_codes[c][:].bitcast(FP8X4),
                        rhs_scale=z_plane[c][:],
                        start=True,
                        stop=True,
                    )

        h_sb = [sb.tile([P, S], F32, name="h_sb%d" % m) for m in range(4)]
        pa = [sb.tile([P, U], F32, name="pa%d" % m) for m in range(4)]
        th = [sb.tile([P, U], F32, name="th%d" % m) for m in range(4)]
        ra2 = [sb.tile([P, U], F32, name="ra2_%d" % m) for m in range(4)]

        def h_out(m):
            nc.scalar.copy(h_sb[m][:], h_banks[m][:])

        def pa_s(m):
            nc.scalar.activation(pa[m][:], h_sb[m][:].indirect(n4_t[:]), COPY)

        def pa_v(m):
            nc.vector.tensor_copy(pa[m][:], h_sb[m][:].indirect(n4_t[:]))

        def tanh(m):
            nc.scalar.activation(th[m][:], pa[m][:], TANH, scale=-1.0)

        def old(m):
            nc.vector.tensor_tensor(ra2[m][:], h_sb[m][:].indirect(n3_t[:]), th[m][:], ADD)

        def put_s(m):
            nc.scalar.activation(h_sb[m][:].indirect(n3_t[:]), ra2[m][:], COPY)
            nc.sync.dma_start(out[m * P : (m + 1) * P, :], h_sb[m][:])

        def put_v(m):
            nc.vector.tensor_copy(h_sb[m][:].indirect(n3_t[:]), ra2[m][:])
            nc.sync.dma_start(out[m * P : (m + 1) * P, :], h_sb[m][:])

        h_out(0)
        pa_v(0)
        h_out(1)
        pa_v(1)
        tanh(0)
        h_out(2)
        old(0)
        tanh(1)
        h_out(3)
        old(1)
        pa_s(2)
        tanh(2)
        put_v(0)
        pa_s(3)
        tanh(3)
        old(2)
        put_s(1)
        old(3)
        put_s(2)
        put_v(3)
